import numpy as np
import ml_dtypes


def mxq(x, axis, fmt="e4m3"):
    dtype, down = {"e4m3": (ml_dtypes.float8_e4m3fn, 7), "e5m2": (ml_dtypes.float8_e5m2, 14)}[fmt]
    v = np.moveaxis(np.asarray(x, np.float32).astype(ml_dtypes.bfloat16).astype(np.float64), axis, -1)
    blocks = v.reshape(v.shape[:-1] + (-1, 32))
    amax = np.abs(blocks).max(-1, keepdims=True)
    byte = np.maximum(np.where(amax > 0, np.frexp(amax)[1] - 1 + 127, 0) - down, 1)
    scale = np.exp2(byte - 127.0)
    codes = (blocks / scale).astype(np.float32).astype(dtype).astype(np.float64)
    return np.moveaxis((codes * scale).reshape(v.shape), -1, axis)


WIDE = False


def mx_kscale(k):
    if not WIDE:
        return np.ones(k)
    levels = np.array([10, -10, 5, -5, 0])
    if k % 512:
        return np.exp2(np.random.permutation(np.resize(levels, k // 32))).repeat(32)
    a = np.empty((k // 512, 16))
    for p in range(k // 512):
        a[p, :8] = np.random.permutation(np.resize(levels, 8))
        for g in range(8):
            far = levels[np.abs(levels - a[p, g]) >= 10]
            a[p, g + 8] = far[np.random.randint(len(far))]
    return np.exp2(a.ravel()).repeat(32)


def f64(x):
    return np.asarray(x).astype(np.float64)


def striped(idx):
    return np.tile(np.asarray(idx).reshape(-1, 16).T, (8, 1)).astype(np.uint16)


def unstriped(offs):
    return offs[:16].T.reshape(-1).astype(np.int64)


E2M1 = np.array([0.0, 0.5, 1.0, 1.5, 2.0, 3.0, 4.0, 6.0, -0.0, -0.5, -1.0, -1.5, -2.0, -3.0, -4.0, -6.0])


def pack_weight(w, fmt):
    k, n = w.shape
    w = f64(np.asarray(w, np.float32).astype(ml_dtypes.bfloat16)).reshape(k // 32, 32, n)
    amax = np.abs(w).max(1)
    if fmt == "e4m3":
        byte = np.frexp(amax)[1] - 1 + 127 - 7
    else:
        mant, ex = np.frexp(amax / 6.0)
        byte = np.where(mant > 0.5, ex, ex - 1) + 127
    byte = np.clip(np.where(amax > 0, byte, 1), 1, 254)
    scaled = (w * np.exp2(127.0 - byte)[:, None, :]).reshape(k, n).astype(np.float32)
    by_word = np.ascontiguousarray(scaled.reshape(k // 512, 128, 4, n).transpose(0, 1, 3, 2))
    if fmt == "e4m3":
        words = by_word.astype(ml_dtypes.float8_e4m3fn).view(np.uint8)
    else:
        c = by_word.astype(ml_dtypes.float4_e2m1fn).view(np.uint8) & 0xF
        words = (c[..., 0::2] | (c[..., 1::2] << 4)).reshape(k // 512, 128, 2 * n)
    return np.ascontiguousarray(words), np.ascontiguousarray(byte.astype(np.uint8).reshape(k // 512, 16, n))


def unpack_weight(words, scales, fmt):
    g, _, n = scales.shape
    words = np.ascontiguousarray(words).reshape(g, 128, n, -1)
    if fmt == "e4m3":
        vals = words.view(ml_dtypes.float8_e4m3fn).astype(np.float64)
    else:
        nib = np.empty((g, 128, n, 4), np.uint8)
        nib[..., 0::2] = words & 0xF
        nib[..., 1::2] = words >> 4
        vals = E2M1[nib]
    vals = vals * np.repeat(np.exp2(scales.astype(np.float64) - 127.0), 8, axis=1)[..., None]
    return vals.transpose(0, 1, 3, 2).reshape(g * 512, n)


def bf(x):
    return np.asarray(x, np.float32).astype(ml_dtypes.bfloat16)


def planes(Y):
    r, m = Y.shape
    b = f64(bf(Y)).reshape(r // 32, 32, m)
    amax = np.abs(b).max(1)
    byte = np.clip(np.where(amax > 0, np.frexp(amax)[1] - 1 + 127 - 7, 1), 1, 254)
    codes = (b * np.exp2(127.0 - byte)[:, None, :]).reshape(r, m).astype(np.float32).astype(ml_dtypes.float8_e4m3fn).view(np.uint8)
    words = codes.reshape(r // 512, 128, 4, m).transpose(0, 1, 3, 2)
    return np.ascontiguousarray(words), np.ascontiguousarray(byte.astype(np.uint8).reshape(r // 512, 16, m))


D, T, I, Q, E = 512, 2048, 512, 256, 512


def setup_inputs():
    n = np.random.standard_normal
    idx = np.random.permutation(T)[:I]
    fd = mx_kscale(D)
    fi = mx_kscale(I)
    ti = np.ones(T)
    ti[idx] = fi
    keysp = pack_weight(n((D, T)) / fd[:, None], "e2m1")
    return {
        "query": (n((D, Q)) * 1.0 / np.sqrt(D) * fd[:, None]).astype(np.float32),
        "keys_words": keysp[0],
        "keys_scales": keysp[1],
        "steep": (np.random.uniform(0.7, 2.0, (Q, 1))).astype(np.float32),
        "base0": (np.random.uniform(-0.5, 0.5, (Q, 1))).astype(np.float32),
        "size": (np.random.uniform(2.0, 8.0, (1, I)) * fi).astype(np.float32),
        "vals": (n((E, T)) / ti).astype(np.float32),
        "offs": striped(idx),
    }


def reference(query, keys_words, keys_scales, steep, base0, size, vals, offs):
    idx = unstriped(offs)
    keysu = unpack_weight(keys_words, keys_scales, "e2m1")
    queryq = mxq(f64(query), 0, "e4m3")
    keysidxg = keysu[:, idx]
    a = queryq.T @ keysidxg
    p = np.tanh(a * f64(steep)) - f64(base0)
    w = p * f64(size) / np.sum(np.abs(p), axis=1, keepdims=True)
    wt = w.T
    vt = f64(vals)[:, idx].T
    vtq = mxq(vt, 0, "e4m3")
    wtq = mxq(wt, 0, "e4m3")
    o = vtq.T @ wtq
    words, scales = planes(o)
    return o, words, scales

@@ -1,0 +1,188 @@
+from contextlib import ExitStack
+
+import concourse.mybir as mybir
+from concourse.masks import make_identity
+
+D, T, I, Q, E = 512, 2048, 512, 256, 512
+FLOPS = 2 * D * Q * I + 2 * I * E * Q
+
+F32 = mybir.dt.float32
+BF16 = mybir.dt.bfloat16
+I32 = mybir.dt.int32
+U32 = mybir.dt.uint32
+U16 = mybir.dt.uint16
+U8 = mybir.dt.uint8
+FP8X4 = mybir.dt.float8_e4m3fn_x4
+FP4X4 = mybir.dt.float4_e2m1fn_x4
+ACT = mybir.ActivationFunctionType
+ALU = mybir.AluOpType
+
+P = 128
+PACK = 4
+HALVES = Q // P
+
+
+def tile_attend_signedread_pl_kernel(tc, query, keys_words, keys_scales, steep, base0, size, vals, offs, out_0, out_1, out_2):
+    nc = tc.nc
+    with ExitStack() as ctx:
+        sb = ctx.enter_context(tc.tile_pool(name="sb", bufs=1))
+        ps = ctx.enter_context(tc.psum_pool(name="ps", bufs=1))
+
+        def tile(name, shape, dtype):
+            return sb.tile(shape, dtype, name=name, align_bytes=64)
+
+        offsets = sb.tile([P, I // 16], U16, name="offsets")
+        nc.sync.dma_start(offsets[:], offs)
+
+        key_scale_pool = tile("key_scale_pool", [P, T], U8)
+        nc.vector.memset(key_scale_pool[:].bitcast(I32), 0)
+        warm = tile("warm", [P, 1], F32)
+        nc.vector.memset(warm[:], 0.0)
+        warm_out = tile("warm_out", [P, 1], F32)
+        nc.scalar.activation(warm_out[:], warm[:], ACT.Tanh)
+
+        key_word_pool = tile("key_word_pool", [P, T], U16)
+        nc.sync.dma_start(key_word_pool[:].bitcast(I32), keys_words[0].bitcast(I32))
+        for quad in range(4):
+            nc.sync.dma_start(
+                key_scale_pool[32 * quad : 32 * quad + 4, :].bitcast(I32),
+                keys_scales[0, 4 * quad : 4 * quad + 4, :].bitcast(I32),
+            )
+        query_raw = tile("query_raw", [P, PACK, Q], F32)
+        nc.sync.dma_start(query_raw[:], query.rearrange("(p j) q -> p j q", j=PACK))
+
+        val_rows = vals.rearrange("(p t) n -> t p n", t=PACK)
+        val_pool = [tile("val_pool%d" % t, [P, T], F32) for t in range(PACK)]
+        nc.sync.dma_start(val_pool[0][:], val_rows[0])
+
+        steep_sb = tile("steep_sb", [P, HALVES], F32)
+        base_sb = tile("base_sb", [P, HALVES], F32)
+        size_sb = tile("size_sb", [P, PACK], F32)
+        with nc.allow_non_contiguous_dma(reason="one value a query row"):
+            nc.sync.dma_start(steep_sb[:], steep.rearrange("(h m) o -> m (h o)", h=HALVES))
+            nc.sync.dma_start(base_sb[:], base0.rearrange("(h m) o -> m (h o)", h=HALVES))
+        nc.sync.dma_start(size_sb[:], size.rearrange("o (p r) -> (o p) r", r=PACK))
+        for t in range(1, PACK):
+            nc.sync.dma_start(val_pool[t][:], val_rows[t])
+
+        ident = tile("ident", [P, P], F32)
+        make_identity(nc, ident[:])
+
+        key_words = tile("key_words", [P, I], U16)
+        nc.vector.tensor_copy(key_words[:], key_word_pool[:].indirect(offsets[:]))
+        key_scales = tile("key_scales", [P, I], U8)
+        nc.vector.tensor_copy(key_scales[:], key_scale_pool[:].indirect(offsets[:]))
+
+        w_codes, w_scales = [], []
+        q_codes, q_scales = [], []
+        for h in range(HALVES):
+            q_bf = tile("q_bf%d" % h, [P, P, PACK], BF16)
+            nc.scalar.copy(
+                q_bf[:].rearrange("p (c i) j -> p c j i", i=4),
+                query_raw[:, :, h * P : (h + 1) * P].rearrange("p j (c i) -> p c j i", i=4),
+            )
+            codes = tile("q_codes%d" % h, [P, P], U32)
+            scales = tile("q_scales%d" % h, [P, P], U8)
+            nc.vector.quantize_mx(codes[:].bitcast(FP8X4), scales[:], q_bf[:].rearrange("p q j -> p (q j)"))
+            q_codes.append(codes)
+            q_scales.append(scales)
+
+        def weights(h):
+            score = ps.tile([P, I], F32, name="score%d" % h)
+            nc.tensor.matmul_mx(
+                score[:], lhsT=q_codes[h][:].bitcast(FP8X4), lhsT_scale=q_scales[h][:],
+                rhs=key_words[:].bitcast(FP4X4), rhs_scale=key_scales[:], start=True, stop=True,
+            )
+            th = tile("th%d" % h, [P, PACK, P], F32)
+            nc.scalar.activation(
+                th[:], score[:].rearrange("q (s r) -> q r s", r=PACK), ACT.Tanh, scale=steep_sb[:, h : h + 1]
+            )
+            mag = tile("mag%d" % h, [P, PACK, P], BF16)
+            total = tile("total%d" % h, [P, 1], F32)
+            nc.scalar.activation(mag[:], th[:], ACT.Abs, bias=base_sb[:, h : h + 1], scale=-1.0, accum_out=total[:])
+            inv = tile("inv%d" % h, [P, 1], F32)
+            nc.vector.reciprocal(inv[:], total[:])
+            shift = tile("shift%d" % h, [P, 1], F32)
+            nc.vector.tensor_scalar(shift[:], base_sb[:, h : h + 1], inv[:], -1.0, ALU.mult, ALU.mult)
+            normed = tile("normed%d" % h, [P, PACK, P], F32)
+            nc.scalar.activation(normed[:], th[:], ACT.Identity, bias=shift[:], scale=inv[:])
+            turned = ps.tile([P, PACK, P], F32, name="w_turned%d" % h)
+            for r in range(PACK):
+                nc.tensor.transpose(turned[:, r, :], normed[:, r, :], ident[:])
+            w_bf = tile("w_bf%d" % h, [P, P, PACK], BF16)
+            nc.vector.tensor_tensor(
+                w_bf[:], turned[:].rearrange("p r q -> p q r"),
+                size_sb[:].unsqueeze(1).to_broadcast([P, P, PACK]), ALU.mult,
+            )
+            codes = tile("w_codes%d" % h, [P, P], U32)
+            scales = tile("w_scales%d" % h, [P, P], U8)
+            nc.vector.quantize_mx(codes[:].bitcast(FP8X4), scales[:], w_bf[:].rearrange("p q r -> p (q r)"))
+            w_codes.append(codes)
+            w_scales.append(scales)
+
+        v_codes, v_scales = [], []
+
+        def values(t):
+            picked = tile("picked%d" % t, [P, I], BF16)
+            nc.vector.tensor_copy(picked[:], val_pool[t][:].indirect(offsets[:]))
+            pairs = picked[:].bitcast(F32)
+            turned = ps.tile([P, 2, P], F32, name="v_turned%d" % (t % 2))
+            for u in range(2):
+                nc.tensor.transpose(turned[:, u, :], pairs[:, u : I // 2 : 2], ident[:])
+            v_bf = tile("v_bf%d" % t, [P, P * PACK], BF16)
+            nc.scalar.copy(
+                v_bf[:].bitcast(F32).rearrange("p (e u) -> p e u", u=2), turned[:].rearrange("p u e -> p e u")
+            )
+            codes = tile("v_codes%d" % t, [P, P], U32)
+            scales = tile("v_scales%d" % t, [P, P], U8)
+            nc.vector.quantize_mx(codes[:].bitcast(FP8X4), scales[:], v_bf[:])
+            v_codes.append(codes)
+            v_scales.append(scales)
+
+        sums = [ps.tile([P, PACK, P], F32, name="sums%d" % h) for h in range(HALVES)]
+
+        def product(t):
+            for h in range(HALVES):
+                nc.tensor.matmul_mx(
+                    sums[h][:, t, :], lhsT=v_codes[t][:].bitcast(FP8X4), lhsT_scale=v_scales[t][:],
+                    rhs=w_codes[h][:].bitcast(FP8X4), rhs_scale=w_scales[h][:], start=True, stop=True,
+                )
+
+        values(0)
+        weights(0)
+        weights(1)
+        values(1)
+        values(2)
+        for t in range(PACK - 1):
+            product(t)
+
+        out_rows = out_0.rearrange("(p t) q -> p t q", t=PACK)
+        y_early = tile("y_early", [P, PACK - 1, Q], F32)
+        for h in range(HALVES):
+            nc.scalar.copy(y_early[:, :, h * P : (h + 1) * P], sums[h][:, 0 : PACK - 1, :])
+        nc.sync.dma_start(out_rows[:, 0 : PACK - 1, :], y_early[:])
+
+        values(PACK - 1)
+        product(PACK - 1)
+
+        y_codes = tile("y_codes", [P, Q], U32)
+        y_scales = tile("y_scales", [P, Q], U8)
+        y_bf = [tile("y_bf%d" % h, [P, P, PACK], BF16) for h in range(HALVES)]
+        nc.vector.tensor_copy(y_bf[0][:], sums[0][:].rearrange("p t q -> p q t"))
+        nc.scalar.copy(y_bf[1][:], sums[1][:].rearrange("p t q -> p q t"))
+        y_last = tile("y_last", [P, Q], F32)
+        for h in (1, 0):
+            nc.scalar.copy(y_last[:, h * P : (h + 1) * P], sums[h][:, PACK - 1, :])
+        for h in range(HALVES):
+            cols = slice(h * P, (h + 1) * P)
+            nc.vector.quantize_mx(
+                y_codes[:, cols].bitcast(FP8X4), y_scales[:, cols], y_bf[h][:].rearrange("p q t -> p (q t)")
+            )
+        nc.scalar.dma_start(out_rows[:, PACK - 1, :], y_last[:])
+        nc.sync.dma_start(out_1[0].rearrange("p c r -> p (c r)").bitcast(I32), y_codes[:].bitcast(I32))
+        for quad in range(4):
+            queue = nc.sync if quad % 2 == 0 else nc.scalar
+            queue.dma_start(
+                out_2[0, 4 * quad : 4 * quad + 4, :].bitcast(I32),
+                y_scales[32 * quad : 32 * quad + 4, :].bitcast(I32),
+            )

@@ -20,16 +20,27 @@ ALU = mybir.AluOpType
 P = 128
 PACK = 4
 HALVES = Q // P
+QUADS = 4
 
 
 def tile_attend_signedread_pl_kernel(tc, query, keys_words, keys_scales, steep, base0, size, vals, offs, out_0, out_1, out_2):
     nc = tc.nc
     with ExitStack() as ctx:
         sb = ctx.enter_context(tc.tile_pool(name="sb", bufs=1))
+        val_space = ctx.enter_context(tc.tile_pool(name="val_space", bufs=1))
         ps = ctx.enter_context(tc.psum_pool(name="ps", bufs=1))
 
-        def tile(name, shape, dtype):
-            return sb.tile(shape, dtype, name=name, align_bytes=64)
+        def tile(name, shape, dtype, slot=None):
+            return sb.tile(shape, dtype, name=name, tag=slot or name, align_bytes=64)
+
+        def on_val_pool(t, name, shape, dtype, byte=0):
+            return val_space.tile(shape, dtype, name=name, align_bytes=64, offset=t * T * 4 + byte)
+
+        def quantise(codes, scales, values):
+            nc.vector.quantize_mx(codes.bitcast(FP8X4), scales, values)
+
+        def half(h):
+            return slice(h * P, (h + 1) * P)
 
         offsets = sb.tile([P, I // 16], U16, name="offsets")
         nc.sync.dma_start(offsets[:], offs)
@@ -41,105 +52,153 @@ def tile_attend_signedread_pl_kernel(tc, query, keys_words, keys_scales, steep, 
         warm_out = tile("warm_out", [P, 1], F32)
         nc.scalar.activation(warm_out[:], warm[:], ACT.Tanh)
 
+        row_consts = tile("row_consts", [P, P], F32)
+        nc.gpsimd.memset(row_consts[:], 0.0)
+        size_row = tile("size_row", [P, I], F32)
+        nc.gpsimd.memset(size_row[:], 0.0)
+        ident = tile("ident", [P, P], F32)
+        make_identity(nc, ident[:])
+
+        nc.sync.dma_start(row_consts[0:HALVES, :], steep.rearrange("(h m) o -> h (m o)", h=HALVES))
         key_word_pool = tile("key_word_pool", [P, T], U16)
         nc.sync.dma_start(key_word_pool[:].bitcast(I32), keys_words[0].bitcast(I32))
-        for quad in range(4):
+        for quad in range(QUADS):
             nc.sync.dma_start(
                 key_scale_pool[32 * quad : 32 * quad + 4, :].bitcast(I32),
                 keys_scales[0, 4 * quad : 4 * quad + 4, :].bitcast(I32),
             )
         query_raw = tile("query_raw", [P, PACK, Q], F32)
         nc.sync.dma_start(query_raw[:], query.rearrange("(p j) q -> p j q", j=PACK))
-
+        nc.sync.dma_start(row_consts[HALVES : 2 * HALVES, :], base0.rearrange("(h m) o -> h (m o)", h=HALVES))
         val_rows = vals.rearrange("(p t) n -> t p n", t=PACK)
-        val_pool = [tile("val_pool%d" % t, [P, T], F32) for t in range(PACK)]
+        val_pool = [on_val_pool(t, "val_pool%d" % t, [P, T], F32) for t in range(PACK)]
         nc.sync.dma_start(val_pool[0][:], val_rows[0])
-
-        steep_sb = tile("steep_sb", [P, HALVES], F32)
-        base_sb = tile("base_sb", [P, HALVES], F32)
-        size_sb = tile("size_sb", [P, PACK], F32)
-        with nc.allow_non_contiguous_dma(reason="one value a query row"):
-            nc.sync.dma_start(steep_sb[:], steep.rearrange("(h m) o -> m (h o)", h=HALVES))
-            nc.sync.dma_start(base_sb[:], base0.rearrange("(h m) o -> m (h o)", h=HALVES))
-        nc.sync.dma_start(size_sb[:], size.rearrange("o (p r) -> (o p) r", r=PACK))
+        nc.sync.dma_start(size_row[0:1, :], size)
         for t in range(1, PACK):
             nc.sync.dma_start(val_pool[t][:], val_rows[t])
 
-        ident = tile("ident", [P, P], F32)
-        make_identity(nc, ident[:])
+        consts_turned = ps.tile([P, P], F32, name="consts_turned", tag="w_turned0")
+        nc.tensor.transpose(consts_turned[:], row_consts[:], ident[:])
 
         key_words = tile("key_words", [P, I], U16)
         nc.vector.tensor_copy(key_words[:], key_word_pool[:].indirect(offsets[:]))
         key_scales = tile("key_scales", [P, I], U8)
         nc.vector.tensor_copy(key_scales[:], key_scale_pool[:].indirect(offsets[:]))
 
-        w_codes, w_scales = [], []
-        q_codes, q_scales = [], []
+        scores = []
         for h in range(HALVES):
             q_bf = tile("q_bf%d" % h, [P, P, PACK], BF16)
             nc.scalar.copy(
                 q_bf[:].rearrange("p (c i) j -> p c j i", i=4),
-                query_raw[:, :, h * P : (h + 1) * P].rearrange("p j (c i) -> p c j i", i=4),
+                query_raw[:, :, half(h)].rearrange("p j (c i) -> p c j i", i=4),
             )
-            codes = tile("q_codes%d" % h, [P, P], U32)
-            scales = tile("q_scales%d" % h, [P, P], U8)
-            nc.vector.quantize_mx(codes[:].bitcast(FP8X4), scales[:], q_bf[:].rearrange("p q j -> p (q j)"))
-            q_codes.append(codes)
-            q_scales.append(scales)
-
-        def weights(h):
-            score = ps.tile([P, I], F32, name="score%d" % h)
+            q_codes = tile("q_codes%d" % h, [P, P], U32, "row_consts" if h == 0 else None)
+            q_scales = tile("q_scales%d" % h, [P, P], U8)
+            quantise(q_codes[:], q_scales[:], q_bf[:].rearrange("p q j -> p (q j)"))
+            score = ps.tile([P, I], F32, name="score%d" % h, tag="score%d" % h)
             nc.tensor.matmul_mx(
-                score[:], lhsT=q_codes[h][:].bitcast(FP8X4), lhsT_scale=q_scales[h][:],
+                score[:], lhsT=q_codes[:].bitcast(FP8X4), lhsT_scale=q_scales[:],
                 rhs=key_words[:].bitcast(FP4X4), rhs_scale=key_scales[:], start=True, stop=True,
             )
-            th = tile("th%d" % h, [P, PACK, P], F32)
-            nc.scalar.activation(
-                th[:], score[:].rearrange("q (s r) -> q r s", r=PACK), ACT.Tanh, scale=steep_sb[:, h : h + 1]
-            )
-            mag = tile("mag%d" % h, [P, PACK, P], BF16)
-            total = tile("total%d" % h, [P, 1], F32)
-            nc.scalar.activation(mag[:], th[:], ACT.Abs, bias=base_sb[:, h : h + 1], scale=-1.0, accum_out=total[:])
-            inv = tile("inv%d" % h, [P, 1], F32)
-            nc.vector.reciprocal(inv[:], total[:])
-            shift = tile("shift%d" % h, [P, 1], F32)
-            nc.vector.tensor_scalar(shift[:], base_sb[:, h : h + 1], inv[:], -1.0, ALU.mult, ALU.mult)
-            normed = tile("normed%d" % h, [P, PACK, P], F32)
-            nc.scalar.activation(normed[:], th[:], ACT.Identity, bias=shift[:], scale=inv[:])
-            turned = ps.tile([P, PACK, P], F32, name="w_turned%d" % h)
-            for r in range(PACK):
-                nc.tensor.transpose(turned[:, r, :], normed[:, r, :], ident[:])
-            w_bf = tile("w_bf%d" % h, [P, P, PACK], BF16)
-            nc.vector.tensor_tensor(
-                w_bf[:], turned[:].rearrange("p r q -> p q r"),
-                size_sb[:].unsqueeze(1).to_broadcast([P, P, PACK]), ALU.mult,
-            )
-            codes = tile("w_codes%d" % h, [P, P], U32)
-            scales = tile("w_scales%d" % h, [P, P], U8)
-            nc.vector.quantize_mx(codes[:].bitcast(FP8X4), scales[:], w_bf[:].rearrange("p q r -> p (q r)"))
-            w_codes.append(codes)
-            w_scales.append(scales)
+            scores.append(score)
 
-        v_codes, v_scales = [], []
+        col_consts = tile("col_consts", [P, 2 * HALVES], F32, "query_raw")
+        nc.scalar.copy(col_consts[:], consts_turned[:, 0 : 2 * HALVES])
+        steep_col = [col_consts[:, h : h + 1] for h in range(HALVES)]
+        base_col = [col_consts[:, HALVES + h : HALVES + h + 1] for h in range(HALVES)]
 
-        def values(t):
-            picked = tile("picked%d" % t, [P, I], BF16)
-            nc.vector.tensor_copy(picked[:], val_pool[t][:].indirect(offsets[:]))
-            pairs = picked[:].bitcast(F32)
-            turned = ps.tile([P, 2, P], F32, name="v_turned%d" % (t % 2))
+        picked, v_bf, v_codes, v_scales = {}, {}, {}, {}
+
+        def gather_values(t):
+            picked[t] = tile("picked%d" % t, [P, I], BF16)
+            nc.vector.tensor_copy(picked[t][:], val_pool[t][:].indirect(offsets[:]))
+
+        def turn_values(t, bank, slot=None):
+            pairs = picked[t][:].bitcast(F32)
+            turned = ps.tile([P, 2, P], F32, name="v_turned%d" % t, tag=bank)
             for u in range(2):
                 nc.tensor.transpose(turned[:, u, :], pairs[:, u : I // 2 : 2], ident[:])
-            v_bf = tile("v_bf%d" % t, [P, P * PACK], BF16)
+            v_bf[t] = tile("v_bf%d" % t, [P, P * PACK], BF16, slot)
             nc.scalar.copy(
-                v_bf[:].bitcast(F32).rearrange("p (e u) -> p e u", u=2), turned[:].rearrange("p u e -> p e u")
+                v_bf[t][:].bitcast(F32).rearrange("p (e u) -> p e u", u=2), turned[:].rearrange("p u e -> p e u")
             )
-            codes = tile("v_codes%d" % t, [P, P], U32)
-            scales = tile("v_scales%d" % t, [P, P], U8)
-            nc.vector.quantize_mx(codes[:].bitcast(FP8X4), scales[:], v_bf[:])
-            v_codes.append(codes)
-            v_scales.append(scales)
+
+        def quantise_values(t, codes):
+            v_codes[t] = codes
+            v_scales[t] = tile("v_scales%d" % t, [P, P], U8)
+            quantise(v_codes[t][:], v_scales[t][:], v_bf[t][:])
+
+        gather_values(0)
+
+        size_turned = ps.tile([P, PACK, P], F32, name="size_turned", tag="w_turned0")
+        for r in range(PACK):
+            nc.tensor.transpose(size_turned[:, r, :], size_row[:, r:I:PACK], ident[:])
+        size_col = tile("size_col", [P, PACK], F32)
+        nc.vector.tensor_copy(size_col[:], size_turned[:, :, 0])
+
+        def squash(h, slot=None):
+            squashed = tile("squashed%d" % h, [P, PACK, P], F32, slot)
+            nc.scalar.activation(
+                squashed[:], scores[h][:].rearrange("q (s r) -> q r s", r=PACK), ACT.Tanh, scale=steep_col[h]
+            )
+            return squashed
+
+        def abs_total(h, squashed):
+            magnitude = tile("magnitude%d" % h, [P, PACK, P], BF16)
+            total = tile("total%d" % h, [P, 1], F32)
+            nc.scalar.activation(
+                magnitude[:], squashed[:], ACT.Abs, bias=base_col[h], scale=-1.0, accum_out=total[:]
+            )
+            return total
+
+        normed = [tile("normed%d" % h, [P, PACK, P], F32) for h in range(HALVES)]
+        w_bf, w_codes, w_scales = {}, {}, {}
+
+        def turn_weights(h, rounded):
+            turned = ps.tile([P, PACK, P], F32, name="w_turned%d" % h, tag="w_turned%d" % h)
+            for r in range(PACK):
+                nc.tensor.transpose(turned[:, r, :], normed[h][:, r, :], ident[:])
+            w_bf[h] = rounded
+            nc.vector.tensor_tensor(
+                rounded[:], turned[:].rearrange("p r q -> p q r"),
+                size_col[:].unsqueeze(1).to_broadcast([P, P, PACK]), ALU.mult,
+            )
+
+        def quantise_weights(h):
+            w_codes[h] = tile("w_codes%d" % h, [P, P], U32)
+            w_scales[h] = tile("w_scales%d" % h, [P, P], U8)
+            quantise(w_codes[h][:], w_scales[h][:], w_bf[h][:].rearrange("p q r -> p (q r)"))
+
+        squashed0 = squash(0)
+        neg_base1 = tile("neg_base1", [P, 1], F32)
+        nc.scalar.mul(neg_base1[:], base_col[1], -1.0)
+        total0 = abs_total(0, squashed0)
+        inverse0 = on_val_pool(0, "inverse0", [P, 1], F32)
+        nc.vector.reciprocal(inverse0[:], total0[:])
+        nc.vector.tensor_scalar(normed[0][:], squashed0[:], base_col[0], inverse0[:], ALU.subtract, ALU.mult)
+        gather_values(1)
+        squashed1 = squash(1, "magnitude0")
+        total1 = abs_total(1, squashed1)
+        raw1 = tile("raw1", [P, PACK, P], F32)
+        nc.scalar.activation(raw1[:], squashed1[:], ACT.Identity, bias=neg_base1[:])
+        inverse1 = on_val_pool(1, "inverse1", [P, 1], F32)
+        nc.vector.reciprocal(inverse1[:], total1[:])
+        nc.scalar.activation(normed[1][:], raw1[:], ACT.Copy, scale=inverse1[:])
+
+        turn_weights(0, on_val_pool(1, "w_bf0", [P, P, PACK], BF16, 64))
+        turn_values(0, "score0", "magnitude1")
+        turn_values(1, "score1", "raw1")
+        quantise_values(0, tile("v_codes0", [P, P], U32, "picked1"))
+        quantise_weights(0)
+        gather_values(2)
+        turn_weights(1, on_val_pool(2, "w_bf1", [P, P, PACK], BF16))
+        turn_values(2, "v_turned2")
+        quantise_values(1, tile("v_codes1", [P, P], U32, "picked2"))
+        quantise_weights(1)
+        gather_values(3)
 
         sums = [ps.tile([P, PACK, P], F32, name="sums%d" % h) for h in range(HALVES)]
+        out_rows = out_0.rearrange("(p t) q -> p t q", t=PACK)
 
         def product(t):
             for h in range(HALVES):
@@ -148,39 +207,32 @@ def tile_attend_signedread_pl_kernel(tc, query, keys_words, keys_scales, steep, 
                     rhs=w_codes[h][:].bitcast(FP8X4), rhs_scale=w_scales[h][:], start=True, stop=True,
                 )
 
-        values(0)
-        weights(0)
-        weights(1)
-        values(1)
-        values(2)
-        for t in range(PACK - 1):
-            product(t)
+        def copy_out(t0, t1, order, slot=None):
+            y = tile("y%d" % t0, [P, t1 - t0, Q], F32, slot)
+            for h in order:
+                nc.scalar.copy(y[:, :, half(h)], sums[h][:, t0:t1, :])
+            return y
 
-        out_rows = out_0.rearrange("(p t) q -> p t q", t=PACK)
-        y_early = tile("y_early", [P, PACK - 1, Q], F32)
-        for h in range(HALVES):
-            nc.scalar.copy(y_early[:, :, h * P : (h + 1) * P], sums[h][:, 0 : PACK - 1, :])
-        nc.sync.dma_start(out_rows[:, 0 : PACK - 1, :], y_early[:])
+        product(0)
+        product(1)
+        nc.sync.dma_start(out_rows[:, 0:2, :], copy_out(0, 2, (0, 1))[:])
+        quantise_values(2, on_val_pool(3, "v_codes2", [P, P], U32))
+        product(2)
+        turn_values(3, "v_turned3")
+        quantise_values(3, tile("v_codes3", [P, P], U32))
+        nc.sync.dma_start(out_rows[:, 2:3, :], copy_out(2, 3, (0, 1), "picked3")[:])
+        product(3)
 
-        values(PACK - 1)
-        product(PACK - 1)
-
+        y_bf = tile("y_bf", [P, Q, PACK], BF16)
+        nc.vector.tensor_copy(y_bf[:, half(0), :], sums[0][:].rearrange("p t q -> p q t"))
+        nc.scalar.copy(y_bf[:, half(1), :], sums[1][:].rearrange("p t q -> p q t"))
+        y_last = copy_out(3, 4, (1, 0))
         y_codes = tile("y_codes", [P, Q], U32)
         y_scales = tile("y_scales", [P, Q], U8)
-        y_bf = [tile("y_bf%d" % h, [P, P, PACK], BF16) for h in range(HALVES)]
-        nc.vector.tensor_copy(y_bf[0][:], sums[0][:].rearrange("p t q -> p q t"))
-        nc.scalar.copy(y_bf[1][:], sums[1][:].rearrange("p t q -> p q t"))
-        y_last = tile("y_last", [P, Q], F32)
-        for h in (1, 0):
-            nc.scalar.copy(y_last[:, h * P : (h + 1) * P], sums[h][:, PACK - 1, :])
-        for h in range(HALVES):
-            cols = slice(h * P, (h + 1) * P)
-            nc.vector.quantize_mx(
-                y_codes[:, cols].bitcast(FP8X4), y_scales[:, cols], y_bf[h][:].rearrange("p q t -> p (q t)")
-            )
-        nc.scalar.dma_start(out_rows[:, PACK - 1, :], y_last[:])
+        quantise(y_codes[:], y_scales[:], y_bf[:].rearrange("p q t -> p (q t)"))
+        nc.scalar.dma_start(out_rows[:, 3:4, :], y_last[:])
         nc.sync.dma_start(out_1[0].rearrange("p c r -> p (c r)").bitcast(I32), y_codes[:].bitcast(I32))
-        for quad in range(4):
+        for quad in range(QUADS):
             queue = nc.sync if quad % 2 == 0 else nc.scalar
             queue.dma_start(
                 out_2[0, 4 * quad : 4 * quad + 4, :].bitcast(I32),

@@ -18,26 +18,31 @@ ACT = mybir.ActivationFunctionType
 ALU = mybir.AluOpType
 
 P = 128
-PACK = 4
+PLACES = 4
 HALVES = Q // P
-QUADS = 4
+QUADRANTS = 4
+ALIGN = 64
+VAL_POOL_BYTES = T * 4
+ROUNDED_BYTES = P * PLACES * 2
 
 
-def tile_attend_signedread_pl_kernel(tc, query, keys_words, keys_scales, steep, base0, size, vals, offs, out_0, out_1, out_2):
+def tile_attend_signedread_pl_kernel(
+    tc, query, keys_words, keys_scales, steep, base0, size, vals, offs, out_0, out_1, out_2
+):
     nc = tc.nc
     with ExitStack() as ctx:
         sb = ctx.enter_context(tc.tile_pool(name="sb", bufs=1))
         val_space = ctx.enter_context(tc.tile_pool(name="val_space", bufs=1))
         ps = ctx.enter_context(tc.psum_pool(name="ps", bufs=1))
 
-        def tile(name, shape, dtype, slot=None):
-            return sb.tile(shape, dtype, name=name, tag=slot or name, align_bytes=64)
+        def tile(name, shape, dtype, reuse=None):
+            return sb.tile(shape, dtype, name=name, tag=reuse or name, align_bytes=ALIGN)
 
         def on_val_pool(t, name, shape, dtype, byte=0):
-            return val_space.tile(shape, dtype, name=name, align_bytes=64, offset=t * T * 4 + byte)
+            return val_space.tile(shape, dtype, name=name, align_bytes=ALIGN, offset=t * VAL_POOL_BYTES + byte)
 
-        def quantise(codes, scales, values):
-            nc.vector.quantize_mx(codes.bitcast(FP8X4), scales, values)
+        def quantise(codes, scales, rounded):
+            nc.vector.quantize_mx(codes.bitcast(FP8X4), scales, rounded)
 
         def half(h):
             return slice(h * P, (h + 1) * P)
@@ -47,38 +52,30 @@ def tile_attend_signedread_pl_kernel(tc, query, keys_words, keys_scales, steep, 
 
         key_scale_pool = tile("key_scale_pool", [P, T], U8)
         nc.vector.memset(key_scale_pool[:].bitcast(I32), 0)
-        warm = tile("warm", [P, 1], F32)
-        nc.vector.memset(warm[:], 0.0)
-        warm_out = tile("warm_out", [P, 1], F32)
-        nc.scalar.activation(warm_out[:], warm[:], ACT.Tanh)
-
-        row_consts = tile("row_consts", [P, P], F32)
-        nc.gpsimd.memset(row_consts[:], 0.0)
-        size_row = tile("size_row", [P, I], F32)
-        nc.gpsimd.memset(size_row[:], 0.0)
         ident = tile("ident", [P, P], F32)
         make_identity(nc, ident[:])
 
-        nc.sync.dma_start(row_consts[0:HALVES, :], steep.rearrange("(h m) o -> h (m o)", h=HALVES))
         key_word_pool = tile("key_word_pool", [P, T], U16)
         nc.sync.dma_start(key_word_pool[:].bitcast(I32), keys_words[0].bitcast(I32))
-        for quad in range(QUADS):
+        for quad in range(QUADRANTS):
             nc.sync.dma_start(
                 key_scale_pool[32 * quad : 32 * quad + 4, :].bitcast(I32),
                 keys_scales[0, 4 * quad : 4 * quad + 4, :].bitcast(I32),
             )
-        query_raw = tile("query_raw", [P, PACK, Q], F32)
-        nc.sync.dma_start(query_raw[:], query.rearrange("(p j) q -> p j q", j=PACK))
-        nc.sync.dma_start(row_consts[HALVES : 2 * HALVES, :], base0.rearrange("(h m) o -> h (m o)", h=HALVES))
-        val_rows = vals.rearrange("(p t) n -> t p n", t=PACK)
-        val_pool = [on_val_pool(t, "val_pool%d" % t, [P, T], F32) for t in range(PACK)]
-        nc.sync.dma_start(val_pool[0][:], val_rows[0])
-        nc.sync.dma_start(size_row[0:1, :], size)
-        for t in range(1, PACK):
+        query_raw = tile("query_raw", [P, PLACES, Q], F32)
+        nc.sync.dma_start(query_raw[:], query.rearrange("(p r) q -> p r q", r=PLACES))
+        val_rows = vals.rearrange("(m t) n -> t m n", t=PLACES)
+        val_pool = [on_val_pool(t, "val_pool%d" % t, [P, T], F32) for t in range(PLACES)]
+        steep_sb = tile("steep_sb", [P, HALVES], F32)
+        base_sb = tile("base_sb", [P, HALVES], F32)
+        size_sb = tile("size_sb", [P, PLACES], F32)
+        with nc.allow_non_contiguous_dma(reason="one value a query row"):
+            nc.sync.dma_start(steep_sb[:], steep.rearrange("(h m) o -> m (h o)", h=HALVES))
+            nc.sync.dma_start(val_pool[0][:], val_rows[0])
+            nc.sync.dma_start(base_sb[:], base0.rearrange("(h m) o -> m (h o)", h=HALVES))
+        nc.sync.dma_start(size_sb[:], size.rearrange("o (p r) -> (o p) r", r=PLACES))
+        for t in range(1, PLACES):
             nc.sync.dma_start(val_pool[t][:], val_rows[t])
-
-        consts_turned = ps.tile([P, P], F32, name="consts_turned", tag="w_turned0")
-        nc.tensor.transpose(consts_turned[:], row_consts[:], ident[:])
 
         key_words = tile("key_words", [P, I], U16)
         nc.vector.tensor_copy(key_words[:], key_word_pool[:].indirect(offsets[:]))
@@ -87,14 +84,14 @@ def tile_attend_signedread_pl_kernel(tc, query, keys_words, keys_scales, steep, 
 
         scores = []
         for h in range(HALVES):
-            q_bf = tile("q_bf%d" % h, [P, P, PACK], BF16)
+            q_rounded = tile("q_rounded%d" % h, [P, P, PLACES], BF16)
             nc.scalar.copy(
-                q_bf[:].rearrange("p (c i) j -> p c j i", i=4),
-                query_raw[:, :, half(h)].rearrange("p j (c i) -> p c j i", i=4),
+                q_rounded[:].rearrange("p (c n) r -> p c r n", n=4),
+                query_raw[:, :, half(h)].rearrange("p r (c n) -> p c r n", n=4),
             )
-            q_codes = tile("q_codes%d" % h, [P, P], U32, "row_consts" if h == 0 else None)
+            q_codes = tile("q_codes%d" % h, [P, P], U32)
             q_scales = tile("q_scales%d" % h, [P, P], U8)
-            quantise(q_codes[:], q_scales[:], q_bf[:].rearrange("p q j -> p (q j)"))
+            quantise(q_codes[:], q_scales[:], q_rounded[:].rearrange("p q r -> p (q r)"))
             score = ps.tile([P, I], F32, name="score%d" % h, tag="score%d" % h)
             nc.tensor.matmul_mx(
                 score[:], lhsT=q_codes[:].bitcast(FP8X4), lhsT_scale=q_scales[:],
@@ -102,72 +99,65 @@ def tile_attend_signedread_pl_kernel(tc, query, keys_words, keys_scales, steep, 
             )
             scores.append(score)
 
-        col_consts = tile("col_consts", [P, 2 * HALVES], F32, "query_raw")
-        nc.scalar.copy(col_consts[:], consts_turned[:, 0 : 2 * HALVES])
-        steep_col = [col_consts[:, h : h + 1] for h in range(HALVES)]
-        base_col = [col_consts[:, HALVES + h : HALVES + h + 1] for h in range(HALVES)]
+        steep_col = [steep_sb[:, h : h + 1] for h in range(HALVES)]
+        base_col = [base_sb[:, h : h + 1] for h in range(HALVES)]
 
-        picked, v_bf, v_codes, v_scales = {}, {}, {}, {}
+        picked, v_rounded, v_codes, v_scales = {}, {}, {}, {}
 
         def gather_values(t):
             picked[t] = tile("picked%d" % t, [P, I], BF16)
             nc.vector.tensor_copy(picked[t][:], val_pool[t][:].indirect(offsets[:]))
 
-        def turn_values(t, bank, slot=None):
+        def turn_values(t, bank, reuse=None):
             pairs = picked[t][:].bitcast(F32)
             turned = ps.tile([P, 2, P], F32, name="v_turned%d" % t, tag=bank)
             for u in range(2):
                 nc.tensor.transpose(turned[:, u, :], pairs[:, u : I // 2 : 2], ident[:])
-            v_bf[t] = tile("v_bf%d" % t, [P, P * PACK], BF16, slot)
+            v_rounded[t] = tile("v_rounded%d" % t, [P, P * PLACES], BF16, reuse)
             nc.scalar.copy(
-                v_bf[t][:].bitcast(F32).rearrange("p (e u) -> p e u", u=2), turned[:].rearrange("p u e -> p e u")
+                v_rounded[t][:].bitcast(F32).rearrange("p (e u) -> p e u", u=2),
+                turned[:].rearrange("p u e -> p e u"),
             )
 
         def quantise_values(t, codes):
             v_codes[t] = codes
             v_scales[t] = tile("v_scales%d" % t, [P, P], U8)
-            quantise(v_codes[t][:], v_scales[t][:], v_bf[t][:])
+            quantise(v_codes[t][:], v_scales[t][:], v_rounded[t][:])
 
         gather_values(0)
 
-        size_turned = ps.tile([P, PACK, P], F32, name="size_turned", tag="w_turned0")
-        for r in range(PACK):
-            nc.tensor.transpose(size_turned[:, r, :], size_row[:, r:I:PACK], ident[:])
-        size_col = tile("size_col", [P, PACK], F32)
-        nc.vector.tensor_copy(size_col[:], size_turned[:, :, 0])
-
-        def squash(h, slot=None):
-            squashed = tile("squashed%d" % h, [P, PACK, P], F32, slot)
+        def squash(h, reuse=None):
+            squashed = tile("squashed%d" % h, [P, PLACES, P], F32, reuse)
             nc.scalar.activation(
-                squashed[:], scores[h][:].rearrange("q (s r) -> q r s", r=PACK), ACT.Tanh, scale=steep_col[h]
+                squashed[:], scores[h][:].rearrange("q (s r) -> q r s", r=PLACES), ACT.Tanh, scale=steep_col[h]
             )
             return squashed
 
         def abs_total(h, squashed):
-            magnitude = tile("magnitude%d" % h, [P, PACK, P], BF16)
+            magnitude = tile("magnitude%d" % h, [P, PLACES, P], BF16)
             total = tile("total%d" % h, [P, 1], F32)
             nc.scalar.activation(
                 magnitude[:], squashed[:], ACT.Abs, bias=base_col[h], scale=-1.0, accum_out=total[:]
             )
             return total
 
-        normed = [tile("normed%d" % h, [P, PACK, P], F32) for h in range(HALVES)]
-        w_bf, w_codes, w_scales = {}, {}, {}
+        normed = [tile("normed%d" % h, [P, PLACES, P], F32) for h in range(HALVES)]
+        w_rounded, w_codes, w_scales = {}, {}, {}
 
         def turn_weights(h, rounded):
-            turned = ps.tile([P, PACK, P], F32, name="w_turned%d" % h, tag="w_turned%d" % h)
-            for r in range(PACK):
+            turned = ps.tile([P, PLACES, P], F32, name="w_turned%d" % h, tag="w_turned%d" % h)
+            for r in range(PLACES):
                 nc.tensor.transpose(turned[:, r, :], normed[h][:, r, :], ident[:])
-            w_bf[h] = rounded
+            w_rounded[h] = rounded
             nc.vector.tensor_tensor(
-                rounded[:], turned[:].rearrange("p r q -> p q r"),
-                size_col[:].unsqueeze(1).to_broadcast([P, P, PACK]), ALU.mult,
+                rounded[:], turned[:].rearrange("s r q -> s q r"),
+                size_sb[:].unsqueeze(1).to_broadcast([P, P, PLACES]), ALU.mult,
             )
 
         def quantise_weights(h):
             w_codes[h] = tile("w_codes%d" % h, [P, P], U32)
             w_scales[h] = tile("w_scales%d" % h, [P, P], U8)
-            quantise(w_codes[h][:], w_scales[h][:], w_bf[h][:].rearrange("p q r -> p (q r)"))
+            quantise(w_codes[h][:], w_scales[h][:], w_rounded[h][:].rearrange("s q r -> s (q r)"))
 
         squashed0 = squash(0)
         neg_base1 = tile("neg_base1", [P, 1], F32)
@@ -179,60 +169,71 @@ def tile_attend_signedread_pl_kernel(tc, query, keys_words, keys_scales, steep, 
         gather_values(1)
         squashed1 = squash(1, "magnitude0")
         total1 = abs_total(1, squashed1)
-        raw1 = tile("raw1", [P, PACK, P], F32)
+        raw1 = tile("raw1", [P, PLACES, P], F32)
         nc.scalar.activation(raw1[:], squashed1[:], ACT.Identity, bias=neg_base1[:])
         inverse1 = on_val_pool(1, "inverse1", [P, 1], F32)
         nc.vector.reciprocal(inverse1[:], total1[:])
         nc.scalar.activation(normed[1][:], raw1[:], ACT.Copy, scale=inverse1[:])
 
-        turn_weights(0, on_val_pool(1, "w_bf0", [P, P, PACK], BF16, 64))
+        turn_weights(0, on_val_pool(1, "w_rounded0", [P, P, PLACES], BF16, ALIGN))
         turn_values(0, "score0", "magnitude1")
         turn_values(1, "score1", "raw1")
         quantise_values(0, tile("v_codes0", [P, P], U32, "picked1"))
         quantise_weights(0)
         gather_values(2)
-        turn_weights(1, on_val_pool(2, "w_bf1", [P, P, PACK], BF16))
+        quantise_values(1, on_val_pool(2, "v_codes1", [P, P], U32))
         turn_values(2, "v_turned2")
-        quantise_values(1, tile("v_codes1", [P, P], U32, "picked2"))
-        quantise_weights(1)
         gather_values(3)
 
-        sums = [ps.tile([P, PACK, P], F32, name="sums%d" % h) for h in range(HALVES)]
-        out_rows = out_0.rearrange("(p t) q -> p t q", t=PACK)
+        sums0 = ps.tile([P, PLACES, P], F32, name="sums0")
+        sums1 = [ps.tile([P, 2, P], F32, name="sums1_%d" % pair, tag="score%d" % pair) for pair in range(2)]
+        out_rows = out_0.rearrange("(m t) q -> m t q", t=PLACES)
+        y_rounded = tile("y_rounded", [P, Q, PLACES], BF16)
 
-        def product(t):
-            for h in range(HALVES):
-                nc.tensor.matmul_mx(
-                    sums[h][:, t, :], lhsT=v_codes[t][:].bitcast(FP8X4), lhsT_scale=v_scales[t][:],
-                    rhs=w_codes[h][:].bitcast(FP8X4), rhs_scale=w_scales[h][:], start=True, stop=True,
-                )
+        def product(t, h):
+            nc.tensor.matmul_mx(
+                sums0[:, t, :] if h == 0 else sums1[t // 2][:, t % 2, :],
+                lhsT=v_codes[t][:].bitcast(FP8X4), lhsT_scale=v_scales[t][:],
+                rhs=w_codes[h][:].bitcast(FP8X4), rhs_scale=w_scales[h][:], start=True, stop=True,
+            )
 
-        def copy_out(t0, t1, order, slot=None):
-            y = tile("y%d" % t0, [P, t1 - t0, Q], F32, slot)
-            for h in order:
-                nc.scalar.copy(y[:, :, half(h)], sums[h][:, t0:t1, :])
-            return y
+        def store_pair(h, pair, copy, queue):
+            places = slice(2 * pair, 2 * pair + 2)
+            y = tile("y%d_%d" % (h, pair), [P, 2, P], F32)
+            copy(y[:], sums0[:, places, :] if h == 0 else sums1[pair][:])
+            queue.dma_start(out_rows[:, places, half(h)], y[:])
 
-        product(0)
-        product(1)
-        nc.sync.dma_start(out_rows[:, 0:2, :], copy_out(0, 2, (0, 1))[:])
-        quantise_values(2, on_val_pool(3, "v_codes2", [P, P], U32))
-        product(2)
+        def round_pair_of_half1(pair):
+            nc.scalar.copy(
+                y_rounded[:, half(1), 2 * pair : 2 * pair + 2], sums1[pair][:].rearrange("m t q -> m q t")
+            )
+
+        product(0, 0)
+        product(1, 0)
+        store_pair(0, 0, nc.scalar.copy, nc.sync)
         turn_values(3, "v_turned3")
+        turn_weights(1, on_val_pool(3, "w_rounded1", [P, P, PLACES], BF16))
+        quantise_values(2, on_val_pool(3, "v_codes2", [P, P], U32, ROUNDED_BYTES))
+        quantise_weights(1)
         quantise_values(3, tile("v_codes3", [P, P], U32))
-        nc.sync.dma_start(out_rows[:, 2:3, :], copy_out(2, 3, (0, 1), "picked3")[:])
-        product(3)
+        product(0, 1)
+        product(1, 1)
+        store_pair(1, 0, nc.scalar.copy, nc.sync)
+        round_pair_of_half1(0)
+        product(2, 0)
+        product(2, 1)
+        product(3, 1)
+        product(3, 0)
 
-        y_bf = tile("y_bf", [P, Q, PACK], BF16)
-        nc.vector.tensor_copy(y_bf[:, half(0), :], sums[0][:].rearrange("p t q -> p q t"))
-        nc.scalar.copy(y_bf[:, half(1), :], sums[1][:].rearrange("p t q -> p q t"))
-        y_last = copy_out(3, 4, (1, 0))
+        round_pair_of_half1(1)
+        nc.vector.tensor_copy(y_rounded[:, half(0), :], sums0[:].rearrange("m t q -> m q t"))
+        store_pair(1, 1, nc.scalar.copy, nc.scalar)
+        store_pair(0, 1, nc.vector.tensor_copy, nc.sync)
         y_codes = tile("y_codes", [P, Q], U32)
         y_scales = tile("y_scales", [P, Q], U8)
-        quantise(y_codes[:], y_scales[:], y_bf[:].rearrange("p q t -> p (q t)"))
-        nc.scalar.dma_start(out_rows[:, 3:4, :], y_last[:])
-        nc.sync.dma_start(out_1[0].rearrange("p c r -> p (c r)").bitcast(I32), y_codes[:].bitcast(I32))
-        for quad in range(QUADS):
+        quantise(y_codes[:], y_scales[:], y_rounded[:].rearrange("m q t -> m (q t)"))
+        nc.sync.dma_start(out_1[0].rearrange("m q t -> m (q t)").bitcast(I32), y_codes[:].bitcast(I32))
+        for quad in range(QUADRANTS):
             queue = nc.sync if quad % 2 == 0 else nc.scalar
             queue.dma_start(
                 out_2[0, 4 * quad : 4 * quad + 4, :].bitcast(I32),

from contextlib import ExitStack

import concourse.mybir as mybir
from concourse.masks import make_identity

D, T, I, Q, E = 512, 2048, 512, 256, 512
FLOPS = 2 * D * Q * I + 2 * I * E * Q

F32 = mybir.dt.float32
BF16 = mybir.dt.bfloat16
I32 = mybir.dt.int32
U32 = mybir.dt.uint32
U16 = mybir.dt.uint16
U8 = mybir.dt.uint8
FP8X4 = mybir.dt.float8_e4m3fn_x4
FP4X4 = mybir.dt.float4_e2m1fn_x4
ACT = mybir.ActivationFunctionType
ALU = mybir.AluOpType

P = 128
PLACES = 4
HALVES = Q // P
QUADRANTS = 4
ALIGN = 64
VAL_POOL_BYTES = T * 4
ROUNDED_BYTES = P * PLACES * 2


def tile_attend_signedread_pl_kernel(
    tc, query, keys_words, keys_scales, steep, base0, size, vals, offs, out_0, out_1, out_2
):
    nc = tc.nc
    with ExitStack() as ctx:
        sb = ctx.enter_context(tc.tile_pool(name="sb", bufs=1))
        val_space = ctx.enter_context(tc.tile_pool(name="val_space", bufs=1))
        ps = ctx.enter_context(tc.psum_pool(name="ps", bufs=1))

        def tile(name, shape, dtype, reuse=None):
            return sb.tile(shape, dtype, name=name, tag=reuse or name, align_bytes=ALIGN)

        def on_val_pool(t, name, shape, dtype, byte=0):
            return val_space.tile(shape, dtype, name=name, align_bytes=ALIGN, offset=t * VAL_POOL_BYTES + byte)

        def quantise(codes, scales, rounded):
            nc.vector.quantize_mx(codes.bitcast(FP8X4), scales, rounded)

        def half(h):
            return slice(h * P, (h + 1) * P)

        offsets = sb.tile([P, I // 16], U16, name="offsets")
        nc.sync.dma_start(offsets[:], offs)

        key_scale_pool = tile("key_scale_pool", [P, T], U8)
        nc.vector.memset(key_scale_pool[:].bitcast(I32), 0)
        ident = tile("ident", [P, P], F32)
        make_identity(nc, ident[:])

        key_word_pool = tile("key_word_pool", [P, T], U16)
        nc.sync.dma_start(key_word_pool[:].bitcast(I32), keys_words[0].bitcast(I32))
        for quad in range(QUADRANTS):
            nc.sync.dma_start(
                key_scale_pool[32 * quad : 32 * quad + 4, :].bitcast(I32),
                keys_scales[0, 4 * quad : 4 * quad + 4, :].bitcast(I32),
            )
        query_raw = tile("query_raw", [P, PLACES, Q], F32)
        nc.sync.dma_start(query_raw[:], query.rearrange("(p r) q -> p r q", r=PLACES))
        val_rows = vals.rearrange("(m t) n -> t m n", t=PLACES)
        val_pool = [on_val_pool(t, "val_pool%d" % t, [P, T], F32) for t in range(PLACES)]
        steep_sb = tile("steep_sb", [P, HALVES], F32)
        base_sb = tile("base_sb", [P, HALVES], F32)
        size_sb = tile("size_sb", [P, PLACES], F32)
        with nc.allow_non_contiguous_dma(reason="one value a query row"):
            nc.sync.dma_start(steep_sb[:], steep.rearrange("(h m) o -> m (h o)", h=HALVES))
            nc.sync.dma_start(val_pool[0][:], val_rows[0])
            nc.sync.dma_start(base_sb[:], base0.rearrange("(h m) o -> m (h o)", h=HALVES))
        nc.sync.dma_start(size_sb[:], size.rearrange("o (p r) -> (o p) r", r=PLACES))
        for t in range(1, PLACES):
            nc.sync.dma_start(val_pool[t][:], val_rows[t])

        key_words = tile("key_words", [P, I], U16)
        nc.vector.tensor_copy(key_words[:], key_word_pool[:].indirect(offsets[:]))
        key_scales = tile("key_scales", [P, I], U8)
        nc.vector.tensor_copy(key_scales[:], key_scale_pool[:].indirect(offsets[:]))

        scores = []
        for h in range(HALVES):
            q_rounded = tile("q_rounded%d" % h, [P, P, PLACES], BF16)
            nc.scalar.copy(
                q_rounded[:].rearrange("p (c n) r -> p c r n", n=4),
                query_raw[:, :, half(h)].rearrange("p r (c n) -> p c r n", n=4),
            )
            q_codes = tile("q_codes%d" % h, [P, P], U32)
            q_scales = tile("q_scales%d" % h, [P, P], U8)
            quantise(q_codes[:], q_scales[:], q_rounded[:].rearrange("p q r -> p (q r)"))
            score = ps.tile([P, I], F32, name="score%d" % h, tag="score%d" % h)
            nc.tensor.matmul_mx(
                score[:], lhsT=q_codes[:].bitcast(FP8X4), lhsT_scale=q_scales[:],
                rhs=key_words[:].bitcast(FP4X4), rhs_scale=key_scales[:], start=True, stop=True,
            )
            scores.append(score)

        steep_col = [steep_sb[:, h : h + 1] for h in range(HALVES)]
        base_col = [base_sb[:, h : h + 1] for h in range(HALVES)]

        picked, v_rounded, v_codes, v_scales = {}, {}, {}, {}

        def gather_values(t):
            picked[t] = tile("picked%d" % t, [P, I], BF16)
            nc.vector.tensor_copy(picked[t][:], val_pool[t][:].indirect(offsets[:]))

        def turn_values(t, bank, reuse=None):
            pairs = picked[t][:].bitcast(F32)
            turned = ps.tile([P, 2, P], F32, name="v_turned%d" % t, tag=bank)
            for u in range(2):
                nc.tensor.transpose(turned[:, u, :], pairs[:, u : I // 2 : 2], ident[:])
            v_rounded[t] = tile("v_rounded%d" % t, [P, P * PLACES], BF16, reuse)
            nc.scalar.copy(
                v_rounded[t][:].bitcast(F32).rearrange("p (e u) -> p e u", u=2),
                turned[:].rearrange("p u e -> p e u"),
            )

        def quantise_values(t, codes):
            v_codes[t] = codes
            v_scales[t] = tile("v_scales%d" % t, [P, P], U8)
            quantise(v_codes[t][:], v_scales[t][:], v_rounded[t][:])

        gather_values(0)

        def squash(h, reuse=None):
            squashed = tile("squashed%d" % h, [P, PLACES, P], F32, reuse)
            nc.scalar.activation(
                squashed[:], scores[h][:].rearrange("q (s r) -> q r s", r=PLACES), ACT.Tanh, scale=steep_col[h]
            )
            return squashed

        def abs_total(h, squashed):
            magnitude = tile("magnitude%d" % h, [P, PLACES, P], BF16)
            total = tile("total%d" % h, [P, 1], F32)
            nc.scalar.activation(
                magnitude[:], squashed[:], ACT.Abs, bias=base_col[h], scale=-1.0, accum_out=total[:]
            )
            return total

        normed = [tile("normed%d" % h, [P, PLACES, P], F32) for h in range(HALVES)]
        w_rounded, w_codes, w_scales = {}, {}, {}

        def turn_weights(h, rounded):
            turned = ps.tile([P, PLACES, P], F32, name="w_turned%d" % h, tag="w_turned%d" % h)
            for r in range(PLACES):
                nc.tensor.transpose(turned[:, r, :], normed[h][:, r, :], ident[:])
            w_rounded[h] = rounded
            nc.vector.tensor_tensor(
                rounded[:], turned[:].rearrange("s r q -> s q r"),
                size_sb[:].unsqueeze(1).to_broadcast([P, P, PLACES]), ALU.mult,
            )

        def quantise_weights(h):
            w_codes[h] = tile("w_codes%d" % h, [P, P], U32)
            w_scales[h] = tile("w_scales%d" % h, [P, P], U8)
            quantise(w_codes[h][:], w_scales[h][:], w_rounded[h][:].rearrange("s q r -> s (q r)"))

        squashed0 = squash(0)
        neg_base1 = tile("neg_base1", [P, 1], F32)
        nc.scalar.mul(neg_base1[:], base_col[1], -1.0)
        total0 = abs_total(0, squashed0)
        inverse0 = on_val_pool(0, "inverse0", [P, 1], F32)
        nc.vector.reciprocal(inverse0[:], total0[:])
        nc.vector.tensor_scalar(normed[0][:], squashed0[:], base_col[0], inverse0[:], ALU.subtract, ALU.mult)
        gather_values(1)
        squashed1 = squash(1, "magnitude0")
        total1 = abs_total(1, squashed1)
        raw1 = tile("raw1", [P, PLACES, P], F32)
        nc.scalar.activation(raw1[:], squashed1[:], ACT.Identity, bias=neg_base1[:])
        inverse1 = on_val_pool(1, "inverse1", [P, 1], F32)
        nc.vector.reciprocal(inverse1[:], total1[:])
        nc.scalar.activation(normed[1][:], raw1[:], ACT.Copy, scale=inverse1[:])

        turn_weights(0, on_val_pool(1, "w_rounded0", [P, P, PLACES], BF16, ALIGN))
        turn_values(0, "score0", "magnitude1")
        turn_values(1, "score1", "raw1")
        quantise_values(0, tile("v_codes0", [P, P], U32, "picked1"))
        quantise_weights(0)
        gather_values(2)
        quantise_values(1, on_val_pool(2, "v_codes1", [P, P], U32))
        turn_values(2, "v_turned2")
        gather_values(3)

        sums0 = ps.tile([P, PLACES, P], F32, name="sums0")
        sums1 = [ps.tile([P, 2, P], F32, name="sums1_%d" % pair, tag="score%d" % pair) for pair in range(2)]
        out_rows = out_0.rearrange("(m t) q -> m t q", t=PLACES)
        y_rounded = tile("y_rounded", [P, Q, PLACES], BF16)

        def product(t, h):
            nc.tensor.matmul_mx(
                sums0[:, t, :] if h == 0 else sums1[t // 2][:, t % 2, :],
                lhsT=v_codes[t][:].bitcast(FP8X4), lhsT_scale=v_scales[t][:],
                rhs=w_codes[h][:].bitcast(FP8X4), rhs_scale=w_scales[h][:], start=True, stop=True,
            )

        def store_pair(h, pair, copy, queue):
            places = slice(2 * pair, 2 * pair + 2)
            y = tile("y%d_%d" % (h, pair), [P, 2, P], F32)
            copy(y[:], sums0[:, places, :] if h == 0 else sums1[pair][:])
            queue.dma_start(out_rows[:, places, half(h)], y[:])

        def round_pair_of_half1(pair):
            nc.scalar.copy(
                y_rounded[:, half(1), 2 * pair : 2 * pair + 2], sums1[pair][:].rearrange("m t q -> m q t")
            )

        product(0, 0)
        product(1, 0)
        store_pair(0, 0, nc.scalar.copy, nc.sync)
        turn_values(3, "v_turned3")
        turn_weights(1, on_val_pool(3, "w_rounded1", [P, P, PLACES], BF16))
        quantise_values(2, on_val_pool(3, "v_codes2", [P, P], U32, ROUNDED_BYTES))
        quantise_weights(1)
        quantise_values(3, tile("v_codes3", [P, P], U32))
        product(0, 1)
        product(1, 1)
        store_pair(1, 0, nc.scalar.copy, nc.sync)
        round_pair_of_half1(0)
        product(2, 0)
        product(2, 1)
        product(3, 1)
        product(3, 0)

        round_pair_of_half1(1)
        nc.vector.tensor_copy(y_rounded[:, half(0), :], sums0[:].rearrange("m t q -> m q t"))
        store_pair(1, 1, nc.scalar.copy, nc.scalar)
        store_pair(0, 1, nc.vector.tensor_copy, nc.sync)
        y_codes = tile("y_codes", [P, Q], U32)
        y_scales = tile("y_scales", [P, Q], U8)
        quantise(y_codes[:], y_scales[:], y_rounded[:].rearrange("m q t -> m (q t)"))
        nc.sync.dma_start(out_1[0].rearrange("m q t -> m (q t)").bitcast(I32), y_codes[:].bitcast(I32))
        for quad in range(QUADRANTS):
            queue = nc.sync if quad % 2 == 0 else nc.scalar
            queue.dma_start(
                out_2[0, 4 * quad : 4 * quad + 4, :].bitcast(I32),
                y_scales[32 * quad : 32 * quad + 4, :].bitcast(I32),
            )
